import numpy as np
import ml_dtypes


def mxq(x, axis, fmt="e4m3"):
    dtype, down = {"e4m3": (ml_dtypes.float8_e4m3fn, 7), "e5m2": (ml_dtypes.float8_e5m2, 14)}[fmt]
    v = np.moveaxis(np.asarray(x, np.float32).astype(ml_dtypes.bfloat16).astype(np.float64), axis, -1)
    blocks = v.reshape(v.shape[:-1] + (-1, 32))
    amax = np.abs(blocks).max(-1, keepdims=True)
    byte = np.maximum(np.where(amax > 0, np.frexp(amax)[1] - 1 + 127, 0) - down, 1)
    scale = np.exp2(byte - 127.0)
    codes = (blocks / scale).astype(np.float32).astype(dtype).astype(np.float64)
    return np.moveaxis((codes * scale).reshape(v.shape), -1, axis)


WIDE = False


def mx_kscale(k):
    if not WIDE:
        return np.ones(k)
    levels = np.array([10, -10, 5, -5, 0])
    if k % 512:
        return np.exp2(np.random.permutation(np.resize(levels, k // 32))).repeat(32)
    a = np.empty((k // 512, 16))
    for p in range(k // 512):
        a[p, :8] = np.random.permutation(np.resize(levels, 8))
        for g in range(8):
            far = levels[np.abs(levels - a[p, g]) >= 10]
            a[p, g + 8] = far[np.random.randint(len(far))]
    return np.exp2(a.ravel()).repeat(32)


def f64(x):
    return np.asarray(x).astype(np.float64)


def striped(idx):
    return np.tile(idx.reshape(-1, 16).T, (8, 1)).astype(np.uint16)


def unstriped(offs):
    return offs[:16].T.reshape(-1).astype(np.int64)


K, T, D, S, V, N = 1536, 1024, 2, 768, 384, 256


def setup_inputs():
    n = np.random.standard_normal
    s = mx_kscale(K)[:, None]
    return {
        "xT": (n((K, T)) * s).astype(np.float32),
        "w": (n((D, K, N)) / np.sqrt(D * K) / s[None]).astype(np.float32),
        "b": (0.3 * n((N, 1))).astype(np.float32),
        "offs": striped(np.random.permutation(T)[:S]),
    }


def reference(xT, w, b, offs):
    idx = unstriped(offs)
    xq = mxq(f64(xT)[:, idx], 0, "e4m3")
    wq = mxq(f64(w), 1, "e4m3")
    y = sum(wq[d].T @ xq[:, d * V:(d + 1) * V] for d in range(D))
    y = y + f64(b)
    return y

@@ -1,0 +1,224 @@
+from contextlib import ExitStack
+
+import concourse.mybir as mybir
+
+K, T, D, S, V, N = 1536, 1024, 2, 768, 384, 256
+FLOPS = 2 * N * V * D * K
+
+F32 = mybir.dt.float32
+BF16 = mybir.dt.bfloat16
+U32 = mybir.dt.uint32
+U16 = mybir.dt.uint16
+U8 = mybir.dt.uint8
+FP8X4 = mybir.dt.float8_e4m3fn_x4
+COPY = mybir.ActivationFunctionType.Copy
+IDENTITY = mybir.ActivationFunctionType.Identity
+ADD = mybir.AluOpType.add
+
+P = 128
+PACK = 4
+K_PASS = P * PACK
+PASSES = K // K_PASS
+HALF = 512
+X_SCALAR = {(0, 0): 176, (0, 1): 176, (1, 0): 0, (1, 1): 448, (2, 0): 512, (2, 1): 208}
+W_SCALAR = {(0, 0): 256, (0, 1): 256, (1, 0): 256, (1, 1): 256, (2, 0): 256, (2, 1): 128}
+M_TILES = N // P
+PIECES = ((0, 256), (256, 384))
+
+
+def regroup(dst, raw):
+    return (
+        dst.rearrange("p (c i) t -> p c t i", i=4),
+        raw.rearrange("p t (c i) -> p c t i", i=4),
+    )
+
+
+def tile_picked_merge_lin_bias_sub_e_kernel(tc, xT, w, b, offs, out):
+    nc = tc.nc
+    with ExitStack() as ctx:
+        keep = ctx.enter_context(tc.tile_pool(name="keep", bufs=1))
+        gate = ctx.enter_context(tc.tile_pool(name="gate", bufs=1))
+        psum = ctx.enter_context(tc.psum_pool(name="psum", bufs=1))
+
+        offsets = keep.tile([P, S // 16], U16, name="offsets")
+        bias = keep.tile([P, M_TILES, 1], F32, name="bias")
+        warm = keep.tile([P, 1], F32, name="warm")
+        warmed = keep.tile([P, 1], F32, name="warmed")
+        nc.gpsimd.memset(warm[:], 0.0)
+        nc.scalar.activation(out=warmed[:], in_=warm[:], func=IDENTITY)
+
+        x_scales = gate.tile([P, T], U8, name="scales_then_w", align_bytes=64)
+        nc.gpsimd.memset(x_scales[:], 0)
+
+        x_raw = {}
+        w_raw = {}
+
+        def load_x(c, t0, t1):
+            raw = keep.tile([P, PACK, t1 - t0], F32, name=f"x_raw_{c}_{t0}")
+            rows = xT[c * K_PASS : (c + 1) * K_PASS, t0:t1]
+            nc.sync.dma_start(out=raw[:], in_=rows.rearrange("(p j) w -> p j w", j=PACK))
+            for t in range(t0, t1, HALF):
+                x_raw[c, t // HALF] = raw[:, :, t - t0 : t - t0 + HALF]
+
+        def load_w(c, d):
+            w_raw[c, d] = keep.tile([P, PACK, N], F32, name=f"w_raw_{c}_{d}")
+            rows = w[d, c * K_PASS : (c + 1) * K_PASS, :]
+            nc.sync.dma_start(out=w_raw[c, d][:], in_=rows.rearrange("(p j) n -> p j n", j=PACK))
+
+        load_x(0, 0, HALF)
+        nc.sync.dma_start(offsets[:], offs)
+        nc.scalar.dma_start(out=bias[:], in_=b.rearrange("(c p) o -> p c o", p=P))
+        load_x(0, HALF, T)
+        load_x(1, 0, T)
+        load_x(2, 0, HALF)
+        load_x(2, HALF, T)
+        for c in range(PASSES):
+            for d in range(D):
+                load_w(c, d)
+
+        x_bf = {}
+        for c in range(PASSES):
+            for h in range(2):
+                if (c, h) != (2, 1):
+                    x_bf[c, h] = keep.tile([P, HALF, PACK], BF16, name=f"x_bf_{c}_{h}", align_bytes=64)
+        x_codes = [gate.tile([P, T], U32, name=f"codes_{c}", align_bytes=64) for c in range(2)]
+        g_codes = [keep.tile([P, S], U32, name=f"g_codes_{c}", align_bytes=64) for c in range(PASSES - 1)]
+        g_scales = keep.tile([P, S], U8, name="g_scales", align_bytes=64)
+
+        w_bf = {}
+        w_codes = {}
+        w_scales = {}
+        for c in range(PASSES):
+            for d in range(D):
+                if (c, d) == (1, 1):
+                    w_bf[c, d] = gate.tile([P, N, PACK], BF16, name="gate", align_bytes=64)
+                elif (c, d) == (1, 0):
+                    w_bf[c, d] = gate.tile([P, N, PACK], BF16, name="w_then_codes", align_bytes=64)
+                else:
+                    w_bf[c, d] = keep.tile([P, N, PACK], BF16, name=f"w_bf_{c}_{d}", align_bytes=64)
+                w_scales[c, d] = keep.tile([P, N], U8, name=f"w_scales_{c}_{d}", align_bytes=64)
+
+        def cast(dst, raw, cut, width):
+            if cut > 0:
+                out_view, in_view = regroup(dst[:, :cut, :], raw[:, :, :cut])
+                nc.scalar.activation(out=out_view, in_=in_view, func=COPY)
+            if cut < width:
+                out_view, in_view = regroup(dst[:, cut:, :], raw[:, :, cut:])
+                nc.vector.tensor_copy(out=out_view, in_=in_view)
+
+        def cast_x(c, h):
+            cast(x_bf[c, h], x_raw[c, h], X_SCALAR[c, h], HALF)
+
+        def cast_w(c, d):
+            cast(w_bf[c, d], w_raw[c, d][:], W_SCALAR[c, d], N)
+
+        def quantize_cols(c, t0, grouped):
+            cols = slice(t0, t0 + grouped.shape[1])
+            nc.vector.quantize_mx(
+                out=x_codes[c][:, cols].bitcast(FP8X4),
+                scales=x_scales[4 * c : P, cols],
+                in_=grouped[:].rearrange("p w j -> p (w j)"),
+            )
+
+        def quantize_x(c, h):
+            quantize_cols(c, h * HALF, x_bf[c, h])
+
+        def gather_codes(c):
+            nc.vector.tensor_copy(out=g_codes[c][:], in_=x_codes[c][:].indirect(offsets[:]))
+
+        def quantize_w(c, d, m0=0, m1=N):
+            nc.vector.quantize_mx(
+                out=w_codes[c, d][:, m0:m1].bitcast(FP8X4),
+                scales=w_scales[c, d][:, m0:m1],
+                in_=w_bf[c, d][:, m0:m1, :].rearrange("p n j -> p (n j)"),
+            )
+
+        def gather_scales():
+            nc.vector.tensor_copy(out=g_scales[:], in_=x_scales[:].indirect(offsets[:]))
+
+        acc = {}
+        for m in range(M_TILES):
+            for i, (v0, v1) in enumerate(PIECES):
+                acc[m, i] = psum.tile([P, v1 - v0], F32, name=f"acc_{m}_{i}")
+
+        def multiply(c, d):
+            for m in (1, 0):
+                m_cols = slice(m * P, (m + 1) * P)
+                for i, (v0, v1) in enumerate(PIECES):
+                    v_cols = slice(d * V + v0, d * V + v1)
+                    nc.tensor.matmul_mx(
+                        out=acc[m, i][:],
+                        lhsT=w_codes[c, d][:, m_cols].bitcast(FP8X4),
+                        lhsT_scale=w_scales[c, d][:, m_cols],
+                        rhs=g_codes[c][:, v_cols].bitcast(FP8X4),
+                        rhs_scale=g_scales[4 * c : P, v_cols],
+                        start=(c == 0 and d == 0),
+                        stop=(c == PASSES - 1 and d == D - 1),
+                    )
+
+        cast_x(0, 0)
+        cast_x(0, 1)
+        quantize_x(0, 0)
+        quantize_x(0, 1)
+        gather_codes(0)
+        cast_x(1, 0)
+        cast_x(1, 1)
+        quantize_x(1, 0)
+        quantize_x(1, 1)
+        cast_x(2, 0)
+        gather_codes(1)
+        x_codes.append(gate.tile([P, T], U32, name="codes_then_w", align_bytes=64))
+        quarter = HALF // 2
+        last_a = keep.tile([P, quarter, PACK], BF16, name="last_a", align_bytes=64)
+        last_b = gate.tile([P, quarter, PACK], BF16, name="codes_1", align_bytes=64)
+        cast(last_a, x_raw[2, 1][:, :, :quarter], quarter, quarter)
+        cast(last_b, x_raw[2, 1][:, :, quarter:], 0, quarter)
+        quantize_x(2, 0)
+        quantize_cols(2, HALF + quarter, last_b)
+        quantize_cols(2, HALF, last_a)
+        cast_w(0, 0)
+        cast_w(0, 1)
+        gather_scales()
+        w_early = gate.tile([P, 2 * D * N], U32, name="scales_then_w", align_bytes=64)
+        w_late = keep.tile([P, D * N], U32, name="w_late", align_bytes=64)
+        for d in range(D):
+            w_codes[0, d] = w_early[:, d * N : (d + 1) * N]
+            w_codes[1, d] = w_early[:, (D + d) * N : (D + d + 1) * N]
+            w_codes[2, d] = w_late[:, d * N : (d + 1) * N]
+        quantize_w(0, 0)
+        quantize_w(0, 1)
+        multiply(0, 0)
+        multiply(0, 1)
+        cast_w(1, 0)
+        quantize_w(1, 0)
+        multiply(1, 0)
+        g_codes.append(gate.tile([P, S], U32, name="w_then_codes", align_bytes=64))
+        gather_codes(2)
+        cast_w(1, 1)
+        quantize_w(1, 1)
+        multiply(1, 1)
+        cast_w(2, 0)
+        quantize_w(2, 0)
+        multiply(2, 0)
+        tail = gate.tile([P, P, PACK], BF16, name="gate", align_bytes=64)
+        cast(tail, w_raw[2, 1][:, :, P:], 0, P)
+        cast(w_bf[2, 1], w_raw[2, 1][:, :, :P], P, P)
+        nc.vector.quantize_mx(
+            out=w_codes[2, 1][:, P:N].bitcast(FP8X4),
+            scales=w_scales[2, 1][:, P:N],
+            in_=tail[:].rearrange("p n j -> p (n j)"),
+        )
+        quantize_w(2, 1, 0, P)
+        multiply(2, 1)
+
+        for m in (1, 0):
+            result = keep.tile([P, V], F32, name=f"result_{m}")
+            for i, (v0, v1) in enumerate(PIECES):
+                if m == 1:
+                    nc.scalar.activation(out=result[:, v0:v1], in_=acc[m, i][:], func=IDENTITY, bias=bias[:, m, :])
+                else:
+                    nc.vector.tensor_scalar(
+                        out=result[:, v0:v1], in0=acc[m, i][:], scalar1=bias[:, m, :], scalar2=None, op0=ADD
+                    )
+            queue = nc.scalar if m == 1 else nc.sync
+            queue.dma_start(out=out[m * P : (m + 1) * P, :], in_=result[:])

@@ -19,35 +19,23 @@ P = 128
 PACK = 4
 K_PASS = P * PACK
 PASSES = K // K_PASS
-HALF = 512
-X_SCALAR = {(0, 0): 176, (0, 1): 176, (1, 0): 0, (1, 1): 448, (2, 0): 512, (2, 1): 208}
-W_SCALAR = {(0, 0): 256, (0, 1): 256, (1, 0): 256, (1, 1): 256, (2, 0): 256, (2, 1): 128}
+HALF = T // 2
+X_VECTOR = 544
+RUN = 4
 M_TILES = N // P
 PIECES = ((0, 256), (256, 384))
-
-
-def regroup(dst, raw):
-    return (
-        dst.rearrange("p (c i) t -> p c t i", i=4),
-        raw.rearrange("p t (c i) -> p c t i", i=4),
-    )
 
 
 def tile_picked_merge_lin_bias_sub_e_kernel(tc, xT, w, b, offs, out):
     nc = tc.nc
     with ExitStack() as ctx:
         keep = ctx.enter_context(tc.tile_pool(name="keep", bufs=1))
-        gate = ctx.enter_context(tc.tile_pool(name="gate", bufs=1))
+        turns = ctx.enter_context(tc.tile_pool(name="turns", bufs=1))
         psum = ctx.enter_context(tc.psum_pool(name="psum", bufs=1))
 
         offsets = keep.tile([P, S // 16], U16, name="offsets")
         bias = keep.tile([P, M_TILES, 1], F32, name="bias")
-        warm = keep.tile([P, 1], F32, name="warm")
-        warmed = keep.tile([P, 1], F32, name="warmed")
-        nc.gpsimd.memset(warm[:], 0.0)
-        nc.scalar.activation(out=warmed[:], in_=warm[:], func=IDENTITY)
-
-        x_scales = gate.tile([P, T], U8, name="scales_then_w", align_bytes=64)
+        x_scales = keep.tile([P, T], U8, name="x_scales", align_bytes=64)
         nc.gpsimd.memset(x_scales[:], 0)
 
         x_raw = {}
@@ -57,18 +45,16 @@ def tile_picked_merge_lin_bias_sub_e_kernel(tc, xT, w, b, offs, out):
             raw = keep.tile([P, PACK, t1 - t0], F32, name=f"x_raw_{c}_{t0}")
             rows = xT[c * K_PASS : (c + 1) * K_PASS, t0:t1]
             nc.sync.dma_start(out=raw[:], in_=rows.rearrange("(p j) w -> p j w", j=PACK))
-            for t in range(t0, t1, HALF):
-                x_raw[c, t // HALF] = raw[:, :, t - t0 : t - t0 + HALF]
+            x_raw[c, t0] = raw
 
         def load_w(c, d):
-            w_raw[c, d] = keep.tile([P, PACK, N], F32, name=f"w_raw_{c}_{d}")
+            w_raw[c, d] = turns.tile([P, PACK, N], F32, name=f"w_raw_{c}_{d}", align_bytes=64)
             rows = w[d, c * K_PASS : (c + 1) * K_PASS, :]
             nc.sync.dma_start(out=w_raw[c, d][:], in_=rows.rearrange("(p j) n -> p j n", j=PACK))
 
-        load_x(0, 0, HALF)
+        load_x(0, 0, T)
         nc.sync.dma_start(offsets[:], offs)
         nc.scalar.dma_start(out=bias[:], in_=b.rearrange("(c p) o -> p c o", p=P))
-        load_x(0, HALF, T)
         load_x(1, 0, T)
         load_x(2, 0, HALF)
         load_x(2, HALF, T)
@@ -76,65 +62,62 @@ def tile_picked_merge_lin_bias_sub_e_kernel(tc, xT, w, b, offs, out):
             for d in range(D):
                 load_w(c, d)
 
-        x_bf = {}
-        for c in range(PASSES):
-            for h in range(2):
-                if (c, h) != (2, 1):
-                    x_bf[c, h] = keep.tile([P, HALF, PACK], BF16, name=f"x_bf_{c}_{h}", align_bytes=64)
-        x_codes = [gate.tile([P, T], U32, name=f"codes_{c}", align_bytes=64) for c in range(2)]
-        g_codes = [keep.tile([P, S], U32, name=f"g_codes_{c}", align_bytes=64) for c in range(PASSES - 1)]
+        def views(dst, raw):
+            return (
+                dst.rearrange("p (c i) t -> p c t i", i=RUN),
+                raw.rearrange("p t (c i) -> p c t i", i=RUN),
+            )
+
+        def cast_on_scalar(dst, raw):
+            out_view, in_view = views(dst, raw)
+            nc.scalar.activation(out=out_view, in_=in_view, func=COPY)
+
+        def cast_on_vector(dst, raw):
+            out_view, in_view = views(dst, raw)
+            nc.vector.tensor_copy(out=out_view, in_=in_view)
+
+        def quantize(codes, scales, grouped):
+            nc.vector.quantize_mx(out=codes.bitcast(FP8X4), scales=scales, in_=grouped.rearrange("p w j -> p (w j)"))
+
+        x_bf = [keep.tile([P, T, PACK], BF16, name=f"x_bf_{c}", align_bytes=64) for c in range(PASSES)]
+        x_codes = [keep.tile([P, T], U32, name=f"x_codes_{c}", align_bytes=64) for c in range(PASSES)]
+        g_codes = {}
         g_scales = keep.tile([P, S], U8, name="g_scales", align_bytes=64)
+
+        def cast_x(c, t0, t1, cast):
+            first = HALF if (c, HALF) in x_raw and t0 >= HALF else 0
+            cast(x_bf[c][:, t0:t1, :], x_raw[c, first][:, :, t0 - first : t1 - first])
+
+        def quantize_x(c, t0, t1):
+            quantize(x_codes[c][:, t0:t1], x_scales[4 * c : P, t0:t1], x_bf[c][:, t0:t1, :])
+
+        def gather_pass(c):
+            picked = keep.tile([P, S], U32, name=f"g_codes_{c}", align_bytes=64)
+            nc.vector.tensor_copy(out=picked[:], in_=x_codes[c][:].indirect(offsets[:]))
+            for d in range(D):
+                g_codes[c, d] = picked[:, d * V : (d + 1) * V]
+
+        def gather_piece(c, d, name):
+            picked = turns.tile([P, V], U32, name=name, align_bytes=64)
+            piece = offsets[:, d * V // 16 : (d + 1) * V // 16]
+            nc.vector.tensor_copy(out=picked[:], in_=x_codes[c][:].indirect(piece))
+            g_codes[c, d] = picked[:]
 
         w_bf = {}
         w_codes = {}
         w_scales = {}
-        for c in range(PASSES):
-            for d in range(D):
-                if (c, d) == (1, 1):
-                    w_bf[c, d] = gate.tile([P, N, PACK], BF16, name="gate", align_bytes=64)
-                elif (c, d) == (1, 0):
-                    w_bf[c, d] = gate.tile([P, N, PACK], BF16, name="w_then_codes", align_bytes=64)
-                else:
-                    w_bf[c, d] = keep.tile([P, N, PACK], BF16, name=f"w_bf_{c}_{d}", align_bytes=64)
-                w_scales[c, d] = keep.tile([P, N], U8, name=f"w_scales_{c}_{d}", align_bytes=64)
-
-        def cast(dst, raw, cut, width):
-            if cut > 0:
-                out_view, in_view = regroup(dst[:, :cut, :], raw[:, :, :cut])
-                nc.scalar.activation(out=out_view, in_=in_view, func=COPY)
-            if cut < width:
-                out_view, in_view = regroup(dst[:, cut:, :], raw[:, :, cut:])
-                nc.vector.tensor_copy(out=out_view, in_=in_view)
-
-        def cast_x(c, h):
-            cast(x_bf[c, h], x_raw[c, h], X_SCALAR[c, h], HALF)
 
         def cast_w(c, d):
-            cast(w_bf[c, d], w_raw[c, d][:], W_SCALAR[c, d], N)
+            w_bf[c, d] = keep.tile([P, N, PACK], BF16, name=f"w_bf_{c}_{d}", align_bytes=64)
+            cast_on_scalar(w_bf[c, d][:], w_raw[c, d][:])
 
-        def quantize_cols(c, t0, grouped):
-            cols = slice(t0, t0 + grouped.shape[1])
-            nc.vector.quantize_mx(
-                out=x_codes[c][:, cols].bitcast(FP8X4),
-                scales=x_scales[4 * c : P, cols],
-                in_=grouped[:].rearrange("p w j -> p (w j)"),
-            )
+        def w_tiles(c, d):
+            w_codes[c, d] = keep.tile([P, N], U32, name=f"w_codes_{c}_{d}", align_bytes=64)
+            w_scales[c, d] = keep.tile([P, N], U8, name=f"w_scales_{c}_{d}", align_bytes=64)
 
-        def quantize_x(c, h):
-            quantize_cols(c, h * HALF, x_bf[c, h])
-
-        def gather_codes(c):
-            nc.vector.tensor_copy(out=g_codes[c][:], in_=x_codes[c][:].indirect(offsets[:]))
-
-        def quantize_w(c, d, m0=0, m1=N):
-            nc.vector.quantize_mx(
-                out=w_codes[c, d][:, m0:m1].bitcast(FP8X4),
-                scales=w_scales[c, d][:, m0:m1],
-                in_=w_bf[c, d][:, m0:m1, :].rearrange("p n j -> p (n j)"),
-            )
-
-        def gather_scales():
-            nc.vector.tensor_copy(out=g_scales[:], in_=x_scales[:].indirect(offsets[:]))
+        def quantize_w(c, d):
+            w_tiles(c, d)
+            quantize(w_codes[c, d][:], w_scales[c, d][:], w_bf[c, d][:])
 
         acc = {}
         for m in range(M_TILES):
@@ -145,70 +128,60 @@ def tile_picked_merge_lin_bias_sub_e_kernel(tc, xT, w, b, offs, out):
             for m in (1, 0):
                 m_cols = slice(m * P, (m + 1) * P)
                 for i, (v0, v1) in enumerate(PIECES):
-                    v_cols = slice(d * V + v0, d * V + v1)
                     nc.tensor.matmul_mx(
                         out=acc[m, i][:],
                         lhsT=w_codes[c, d][:, m_cols].bitcast(FP8X4),
                         lhsT_scale=w_scales[c, d][:, m_cols],
-                        rhs=g_codes[c][:, v_cols].bitcast(FP8X4),
-                        rhs_scale=g_scales[4 * c : P, v_cols],
+                        rhs=g_codes[c, d][:, v0:v1].bitcast(FP8X4),
+                        rhs_scale=g_scales[4 * c : P, d * V + v0 : d * V + v1],
                         start=(c == 0 and d == 0),
                         stop=(c == PASSES - 1 and d == D - 1),
                     )
 
-        cast_x(0, 0)
-        cast_x(0, 1)
-        quantize_x(0, 0)
-        quantize_x(0, 1)
-        gather_codes(0)
-        cast_x(1, 0)
-        cast_x(1, 1)
-        quantize_x(1, 0)
-        quantize_x(1, 1)
-        cast_x(2, 0)
-        gather_codes(1)
-        x_codes.append(gate.tile([P, T], U32, name="codes_then_w", align_bytes=64))
-        quarter = HALF // 2
-        last_a = keep.tile([P, quarter, PACK], BF16, name="last_a", align_bytes=64)
-        last_b = gate.tile([P, quarter, PACK], BF16, name="codes_1", align_bytes=64)
-        cast(last_a, x_raw[2, 1][:, :, :quarter], quarter, quarter)
-        cast(last_b, x_raw[2, 1][:, :, quarter:], 0, quarter)
-        quantize_x(2, 0)
-        quantize_cols(2, HALF + quarter, last_b)
-        quantize_cols(2, HALF, last_a)
-        cast_w(0, 0)
-        cast_w(0, 1)
-        gather_scales()
-        w_early = gate.tile([P, 2 * D * N], U32, name="scales_then_w", align_bytes=64)
-        w_late = keep.tile([P, D * N], U32, name="w_late", align_bytes=64)
+        for c in range(2):
+            cast_x(c, 0, X_VECTOR, cast_on_vector)
+            cast_x(c, 768, T, cast_on_scalar)
+            cast_x(c, X_VECTOR, 768, cast_on_scalar)
+            quantize_x(c, 768, T)
+            quantize_x(c, 0, 512)
+            quantize_x(c, 512, 768)
+            if c == 0:
+                gather_pass(c)
+        cast_x(2, 0, 128, cast_on_scalar)
+        quantize_x(2, 0, 128)
+        gather_pass(1)
+        cast_x(2, 128, 256, cast_on_scalar)
+        cast_x(2, 256, 512, cast_on_scalar)
+        quantize_x(2, 128, 256)
+        cast_x(2, 512, 768, cast_on_vector)
+        cast_x(2, 768, T, cast_on_scalar)
+        quantize_x(2, 256, 512)
+        quantize_x(2, 512, 768)
+        quantize_x(2, 768, T)
+        nc.vector.tensor_copy(out=g_scales[:], in_=x_scales[:].indirect(offsets[:]))
+
         for d in range(D):
-            w_codes[0, d] = w_early[:, d * N : (d + 1) * N]
-            w_codes[1, d] = w_early[:, (D + d) * N : (D + d + 1) * N]
-            w_codes[2, d] = w_late[:, d * N : (d + 1) * N]
-        quantize_w(0, 0)
-        quantize_w(0, 1)
-        multiply(0, 0)
-        multiply(0, 1)
+            cast_w(0, d)
+            quantize_w(0, d)
+            multiply(0, d)
+        gather_piece(2, 0, "w_raw_0_1")
         cast_w(1, 0)
         quantize_w(1, 0)
         multiply(1, 0)
-        g_codes.append(gate.tile([P, S], U32, name="w_then_codes", align_bytes=64))
-        gather_codes(2)
-        cast_w(1, 1)
-        quantize_w(1, 1)
-        multiply(1, 1)
-        cast_w(2, 0)
-        quantize_w(2, 0)
-        multiply(2, 0)
-        tail = gate.tile([P, P, PACK], BF16, name="gate", align_bytes=64)
-        cast(tail, w_raw[2, 1][:, :, P:], 0, P)
-        cast(w_bf[2, 1], w_raw[2, 1][:, :, :P], P, P)
-        nc.vector.quantize_mx(
-            out=w_codes[2, 1][:, P:N].bitcast(FP8X4),
-            scales=w_scales[2, 1][:, P:N],
-            in_=tail[:].rearrange("p n j -> p (n j)"),
-        )
-        quantize_w(2, 1, 0, P)
+        gather_piece(2, 1, "w_raw_1_0")
+        for c, d in ((1, 1), (2, 0)):
+            cast_w(c, d)
+            quantize_w(c, d)
+            multiply(c, d)
+
+        w_tiles(2, 1)
+        last = {}
+        for m, cast in ((1, cast_on_vector), (0, cast_on_scalar)):
+            last[m] = keep.tile([P, P, PACK], BF16, name=f"w_last_{m}", align_bytes=64)
+            cast(last[m][:], w_raw[2, 1][:, :, m * P : (m + 1) * P])
+        for m in (1, 0):
+            m_cols = slice(m * P, (m + 1) * P)
+            quantize(w_codes[2, 1][:, m_cols], w_scales[2, 1][:, m_cols], last[m][:])
         multiply(2, 1)
 
         for m in (1, 0):

@@ -54,13 +54,13 @@ def tile_picked_merge_lin_bias_sub_e_kernel(tc, xT, w, b, offs, out):
 
         load_x(0, 0, T)
         nc.sync.dma_start(offsets[:], offs)
-        nc.scalar.dma_start(out=bias[:], in_=b.rearrange("(c p) o -> p c o", p=P))
         load_x(1, 0, T)
         load_x(2, 0, HALF)
         load_x(2, HALF, T)
         for c in range(PASSES):
             for d in range(D):
                 load_w(c, d)
+        nc.sync.dma_start(out=bias[:], in_=b.rearrange("(c p) o -> p c o", p=P))
 
         def views(dst, raw):
             return (
@@ -82,7 +82,7 @@ def tile_picked_merge_lin_bias_sub_e_kernel(tc, xT, w, b, offs, out):
         x_bf = [keep.tile([P, T, PACK], BF16, name=f"x_bf_{c}", align_bytes=64) for c in range(PASSES)]
         x_codes = [keep.tile([P, T], U32, name=f"x_codes_{c}", align_bytes=64) for c in range(PASSES)]
         g_codes = {}
-        g_scales = keep.tile([P, S], U8, name="g_scales", align_bytes=64)
+        g_scales = {}
 
         def cast_x(c, t0, t1, cast):
             first = HALF if (c, HALF) in x_raw and t0 >= HALF else 0
@@ -133,7 +133,7 @@ def tile_picked_merge_lin_bias_sub_e_kernel(tc, xT, w, b, offs, out):
                         lhsT=w_codes[c, d][:, m_cols].bitcast(FP8X4),
                         lhsT_scale=w_scales[c, d][:, m_cols],
                         rhs=g_codes[c, d][:, v0:v1].bitcast(FP8X4),
-                        rhs_scale=g_scales[4 * c : P, d * V + v0 : d * V + v1],
+                        rhs_scale=g_scales[d][4 * c : P, v0:v1],
                         start=(c == 0 and d == 0),
                         stop=(c == PASSES - 1 and d == D - 1),
                     )
@@ -145,39 +145,45 @@ def tile_picked_merge_lin_bias_sub_e_kernel(tc, xT, w, b, offs, out):
             quantize_x(c, 768, T)
             quantize_x(c, 0, 512)
             quantize_x(c, 512, 768)
-            if c == 0:
-                gather_pass(c)
-        cast_x(2, 0, 128, cast_on_scalar)
-        quantize_x(2, 0, 128)
-        gather_pass(1)
-        cast_x(2, 128, 256, cast_on_scalar)
+            gather_pass(c)
+        cast_x(2, 0, 256, cast_on_scalar)
         cast_x(2, 256, 512, cast_on_scalar)
-        quantize_x(2, 128, 256)
+        quantize_x(2, 0, 256)
         cast_x(2, 512, 768, cast_on_vector)
         cast_x(2, 768, T, cast_on_scalar)
         quantize_x(2, 256, 512)
         quantize_x(2, 512, 768)
         quantize_x(2, 768, T)
-        nc.vector.tensor_copy(out=g_scales[:], in_=x_scales[:].indirect(offsets[:]))
 
-        for d in range(D):
-            cast_w(0, d)
-            quantize_w(0, d)
-            multiply(0, d)
+        def gather_scales(d, pool, name):
+            g_scales[d] = pool.tile([P, V], U8, name=name, align_bytes=64)
+            piece = offsets[:, d * V // 16 : (d + 1) * V // 16]
+            nc.vector.tensor_copy(out=g_scales[d][:], in_=x_scales[:].indirect(piece))
+
+        gather_scales(0, keep, "g_scales_0")
+        cast_w(0, 0)
+        quantize_w(0, 0)
+        multiply(0, 0)
+        gather_scales(1, turns, "w_raw_0_0")
+        cast_w(0, 1)
+        quantize_w(0, 1)
+        multiply(0, 1)
         gather_piece(2, 0, "w_raw_0_1")
         cast_w(1, 0)
         quantize_w(1, 0)
         multiply(1, 0)
-        gather_piece(2, 1, "w_raw_1_0")
-        for c, d in ((1, 1), (2, 0)):
-            cast_w(c, d)
-            quantize_w(c, d)
-            multiply(c, d)
+        cast_w(1, 1)
+        quantize_w(1, 1)
+        multiply(1, 1)
+        gather_piece(2, 1, "w_raw_1_1")
+        cast_w(2, 0)
+        quantize_w(2, 0)
+        multiply(2, 0)
 
         w_tiles(2, 1)
         last = {}
-        for m, cast in ((1, cast_on_vector), (0, cast_on_scalar)):
-            last[m] = keep.tile([P, P, PACK], BF16, name=f"w_last_{m}", align_bytes=64)
+        for m, cast, name in ((1, cast_on_scalar, "w_last"), (0, cast_on_vector, "w_raw_2_0")):
+            last[m] = turns.tile([P, P, PACK], BF16, name=name, align_bytes=64)
             cast(last[m][:], w_raw[2, 1][:, :, m * P : (m + 1) * P])
         for m in (1, 0):
             m_cols = slice(m * P, (m + 1) * P)
@@ -187,11 +193,11 @@ def tile_picked_merge_lin_bias_sub_e_kernel(tc, xT, w, b, offs, out):
         for m in (1, 0):
             result = keep.tile([P, V], F32, name=f"result_{m}")
             for i, (v0, v1) in enumerate(PIECES):
-                if m == 1:
+                if m != i:
                     nc.scalar.activation(out=result[:, v0:v1], in_=acc[m, i][:], func=IDENTITY, bias=bias[:, m, :])
                 else:
                     nc.vector.tensor_scalar(
                         out=result[:, v0:v1], in0=acc[m, i][:], scalar1=bias[:, m, :], scalar2=None, op0=ADD
                     )
-            queue = nc.scalar if m == 1 else nc.sync
+            queue = nc.sync if m == 1 else nc.scalar
             queue.dma_start(out=out[m * P : (m + 1) * P, :], in_=result[:])

@@ -1,6 +1,7 @@
 from contextlib import ExitStack
 
 import concourse.mybir as mybir
+from concourse.masks import make_identity
 
 K, T, D, S, V, N = 1536, 1024, 2, 768, 384, 256
 FLOPS = 2 * N * V * D * K
@@ -20,6 +21,7 @@ PACK = 4
 K_PASS = P * PACK
 PASSES = K // K_PASS
 HALF = T // 2
+EARLY = 384
 X_VECTOR = 544
 RUN = 4
 M_TILES = N // P
@@ -34,7 +36,13 @@ def tile_picked_merge_lin_bias_sub_e_kernel(tc, xT, w, b, offs, out):
         psum = ctx.enter_context(tc.psum_pool(name="psum", bufs=1))
 
         offsets = keep.tile([P, S // 16], U16, name="offsets")
-        bias = keep.tile([P, M_TILES, 1], F32, name="bias")
+        bias_rows = keep.tile([P, P], F32, name="bias_rows")
+        nc.gpsimd.memset(bias_rows[:], 0.0)
+        nc.scalar.dma_start(out=bias_rows[:M_TILES, :], in_=b.rearrange("(c p) o -> c (p o)", p=P))
+        identity = keep.tile([P, P], F32, name="identity")
+        make_identity(nc, identity[:])
+        bias_turned = psum.tile([P, P], F32, name="bias_turned")
+        nc.tensor.transpose(bias_turned[:], bias_rows[:], identity[:])
         x_scales = keep.tile([P, T], U8, name="x_scales", align_bytes=64)
         nc.gpsimd.memset(x_scales[:], 0)
 
@@ -42,7 +50,7 @@ def tile_picked_merge_lin_bias_sub_e_kernel(tc, xT, w, b, offs, out):
         w_raw = {}
 
         def load_x(c, t0, t1):
-            raw = keep.tile([P, PACK, t1 - t0], F32, name=f"x_raw_{c}_{t0}")
+            raw = turns.tile([P, PACK, t1 - t0], F32, name=f"x_raw_{c}_{t0}")
             rows = xT[c * K_PASS : (c + 1) * K_PASS, t0:t1]
             nc.sync.dma_start(out=raw[:], in_=rows.rearrange("(p j) w -> p j w", j=PACK))
             x_raw[c, t0] = raw
@@ -55,12 +63,14 @@ def tile_picked_merge_lin_bias_sub_e_kernel(tc, xT, w, b, offs, out):
         load_x(0, 0, T)
         nc.sync.dma_start(offsets[:], offs)
         load_x(1, 0, T)
-        load_x(2, 0, HALF)
-        load_x(2, HALF, T)
+        split = keep.tile([P, 2, 2, 2 * T], F32, name="x_raw_2")
+        rows = xT[2 * K_PASS :, :].rearrange("(p u e) w -> p u (e w)", u=2, e=2)
+        nc.sync.dma_start(out=split[:, 0, :, : T + EARLY], in_=rows[:, :, : T + EARLY])
+        nc.sync.dma_start(out=split[:, 1, :, EARLY:T], in_=rows[:, :, T + EARLY :])
+        x_raw[2, 0] = split[:, 0, :, :].rearrange("p u (e w) -> p (u e) w", e=2)
         for c in range(PASSES):
             for d in range(D):
                 load_w(c, d)
-        nc.sync.dma_start(out=bias[:], in_=b.rearrange("(c p) o -> p c o", p=P))
 
         def views(dst, raw):
             return (
@@ -146,13 +156,25 @@ def tile_picked_merge_lin_bias_sub_e_kernel(tc, xT, w, b, offs, out):
             quantize_x(c, 0, 512)
             quantize_x(c, 512, 768)
             gather_pass(c)
+        bias = turns.tile([P, M_TILES], F32, name="x_raw_1_0")
+        nc.scalar.copy(out=bias[:], in_=bias_turned[:, :M_TILES])
         cast_x(2, 0, 256, cast_on_scalar)
-        cast_x(2, 256, 512, cast_on_scalar)
+        cast_x(2, 256, EARLY, cast_on_scalar)
         quantize_x(2, 0, 256)
-        cast_x(2, 512, 768, cast_on_vector)
-        cast_x(2, 768, T, cast_on_scalar)
-        quantize_x(2, 256, 512)
-        quantize_x(2, 512, 768)
+
+        def late_views(t0, t1):
+            return (
+                x_bf[2][:, t0:t1, :].rearrange("p (c i) (u e) -> p c u e i", i=RUN, e=2),
+                split[:, :, :, t0:t1].rearrange("p e u (c i) -> p c u e i", i=RUN),
+            )
+
+        out_view, in_view = late_views(EARLY, 768)
+        nc.vector.tensor_copy(out=out_view, in_=in_view)
+        out_view, in_view = late_views(768, T)
+        nc.scalar.copy(out=out_view, in_=in_view)
+        quantize_x(2, 256, EARLY)
+        quantize_x(2, EARLY, 640)
+        quantize_x(2, 640, 768)
         quantize_x(2, 768, T)
 
         def gather_scales(d, pool, name):
@@ -191,13 +213,14 @@ def tile_picked_merge_lin_bias_sub_e_kernel(tc, xT, w, b, offs, out):
         multiply(2, 1)
 
         for m in (1, 0):
-            result = keep.tile([P, V], F32, name=f"result_{m}")
             for i, (v0, v1) in enumerate(PIECES):
+                result = keep.tile([P, v1 - v0], F32, name=f"result_{m}_{i}")
                 if m != i:
-                    nc.scalar.activation(out=result[:, v0:v1], in_=acc[m, i][:], func=IDENTITY, bias=bias[:, m, :])
+                    nc.scalar.activation(out=result[:], in_=acc[m, i][:], func=IDENTITY, bias=bias[:, m : m + 1])
+                    queue = nc.scalar
                 else:
                     nc.vector.tensor_scalar(
-                        out=result[:, v0:v1], in0=acc[m, i][:], scalar1=bias[:, m, :], scalar2=None, op0=ADD
+                        out=result[:], in0=acc[m, i][:], scalar1=bias[:, m : m + 1], scalar2=None, op0=ADD
                     )
-            queue = nc.sync if m == 1 else nc.scalar
-            queue.dma_start(out=out[m * P : (m + 1) * P, :], in_=result[:])
+                    queue = nc.sync
+                queue.dma_start(out=out[m * P : (m + 1) * P, v0:v1], in_=result[:])

@@ -23,7 +23,7 @@ PASSES = K // K_PASS
 HALF = T // 2
 EARLY = 384
 X_VECTOR = 544
-RUN = 4
+RUN = 2
 M_TILES = N // P
 PIECES = ((0, 256), (256, 384))
 

@@ -117,9 +117,11 @@ def tile_picked_merge_lin_bias_sub_e_kernel(tc, xT, w, b, offs, out):
         w_codes = {}
         w_scales = {}
 
-        def cast_w(c, d):
+        def cast_w(c, d, cut=N):
             w_bf[c, d] = keep.tile([P, N, PACK], BF16, name=f"w_bf_{c}_{d}", align_bytes=64)
-            cast_on_scalar(w_bf[c, d][:], w_raw[c, d][:])
+            cast_on_scalar(w_bf[c, d][:, :cut, :], w_raw[c, d][:, :, :cut])
+            if cut < N:
+                cast_on_vector(w_bf[c, d][:, cut:, :], w_raw[c, d][:, :, cut:])
 
         def w_tiles(c, d):
             w_codes[c, d] = keep.tile([P, N], U32, name=f"w_codes_{c}_{d}", align_bytes=64)
@@ -198,15 +200,21 @@ def tile_picked_merge_lin_bias_sub_e_kernel(tc, xT, w, b, offs, out):
         quantize_w(1, 1)
         multiply(1, 1)
         gather_piece(2, 1, "w_raw_1_1")
-        cast_w(2, 0)
-        quantize_w(2, 0)
+        w_tiles(2, 0)
+        for m in (1, 0):
+            m_cols = slice(m * P, (m + 1) * P)
+            half = keep.tile([P, P, PACK], BF16, name=f"w_half_{m}", align_bytes=64)
+            cast_on_scalar(half[:], w_raw[2, 0][:, :, m_cols])
+            quantize(w_codes[2, 0][:, m_cols], w_scales[2, 0][:, m_cols], half[:])
         multiply(2, 0)
 
         w_tiles(2, 1)
         last = {}
-        for m, cast, name in ((1, cast_on_scalar, "w_last"), (0, cast_on_vector, "w_raw_2_0")):
+        for m, name in ((1, "w_last"), (0, "w_raw_2_0")):
             last[m] = turns.tile([P, P, PACK], BF16, name=name, align_bytes=64)
-            cast(last[m][:], w_raw[2, 1][:, :, m * P : (m + 1) * P])
+        cast_on_scalar(last[1][:], w_raw[2, 1][:, :, P:])
+        cast_on_vector(last[0][:, :64, :], w_raw[2, 1][:, :, :64])
+        cast_on_scalar(last[0][:, 64:, :], w_raw[2, 1][:, :, 64:P])
         for m in (1, 0):
             m_cols = slice(m * P, (m + 1) * P)
             quantize(w_codes[2, 1][:, m_cols], w_scales[2, 1][:, m_cols], last[m][:])

@@ -62,7 +62,12 @@ def tile_picked_merge_lin_bias_sub_e_kernel(tc, xT, w, b, offs, out):
 
         load_x(0, 0, T)
         nc.sync.dma_start(offsets[:], offs)
-        load_x(1, 0, T)
+        raw = turns.tile([P, PACK * T], F32, name="x_raw_1_0")
+        rows = xT[K_PASS : 2 * K_PASS, :].rearrange("(p j) w -> p (j w)", j=PACK)
+        cut = (PACK - 1) * T + 256
+        nc.sync.dma_start(out=raw[:, :cut], in_=rows[:, :cut])
+        nc.sync.dma_start(out=raw[:, cut:], in_=rows[:, cut:])
+        x_raw[1, 0] = raw[:].rearrange("p (j w) -> p j w", j=PACK)
         split = keep.tile([P, 2, 2, 2 * T], F32, name="x_raw_2")
         rows = xT[2 * K_PASS :, :].rearrange("(p u e) w -> p u (e w)", u=2, e=2)
         nc.sync.dma_start(out=split[:, 0, :, : T + EARLY], in_=rows[:, :, : T + EARLY])
@@ -150,7 +155,7 @@ def tile_picked_merge_lin_bias_sub_e_kernel(tc, xT, w, b, offs, out):
                         stop=(c == PASSES - 1 and d == D - 1),
                     )
 
-        for c in range(2):
+        for c in range(1):
             cast_x(c, 0, X_VECTOR, cast_on_vector)
             cast_x(c, 768, T, cast_on_scalar)
             cast_x(c, X_VECTOR, 768, cast_on_scalar)
@@ -158,6 +163,13 @@ def tile_picked_merge_lin_bias_sub_e_kernel(tc, xT, w, b, offs, out):
             quantize_x(c, 0, 512)
             quantize_x(c, 512, 768)
             gather_pass(c)
+        cast_x(1, 0, 256, cast_on_scalar)
+        cast_x(1, 256, 640, cast_on_vector)
+        cast_x(1, 768, T, cast_on_scalar)
+        cast_x(1, 640, 768, cast_on_scalar)
+        for t0 in (0, 256, 768, 512):
+            quantize_x(1, t0, t0 + 256)
+        gather_pass(1)
         bias = turns.tile([P, M_TILES], F32, name="x_raw_1_0")
         nc.scalar.copy(out=bias[:], in_=bias_turned[:, :M_TILES])
         cast_x(2, 0, 256, cast_on_scalar)

@@ -68,7 +68,7 @@ def tile_picked_merge_lin_bias_sub_e_kernel(tc, xT, w, b, offs, out):
         nc.sync.dma_start(out=raw[:, :cut], in_=rows[:, :cut])
         nc.sync.dma_start(out=raw[:, cut:], in_=rows[:, cut:])
         x_raw[1, 0] = raw[:].rearrange("p (j w) -> p j w", j=PACK)
-        split = keep.tile([P, 2, 2, 2 * T], F32, name="x_raw_2")
+        split = keep.tile([P, 2, 2, 2 * T], F32, name="x_raw_2", align_bytes=64)
         rows = xT[2 * K_PASS :, :].rearrange("(p u e) w -> p u (e w)", u=2, e=2)
         nc.sync.dma_start(out=split[:, 0, :, : T + EARLY], in_=rows[:, :, : T + EARLY])
         nc.sync.dma_start(out=split[:, 1, :, EARLY:T], in_=rows[:, :, T + EARLY :])
@@ -196,8 +196,10 @@ def tile_picked_merge_lin_bias_sub_e_kernel(tc, xT, w, b, offs, out):
             piece = offsets[:, d * V // 16 : (d + 1) * V // 16]
             nc.vector.tensor_copy(out=g_scales[d][:], in_=x_scales[:].indirect(piece))
 
+        w_bf[0, 0] = keep.tile([P, N, PACK], BF16, name="x_raw_2", align_bytes=64)
+        cast_on_vector(w_bf[0, 0][:, :96, :], w_raw[0, 0][:, :, :96])
+        cast_on_scalar(w_bf[0, 0][:, 96:, :], w_raw[0, 0][:, :, 96:])
         gather_scales(0, keep, "g_scales_0")
-        cast_w(0, 0)
         quantize_w(0, 0)
         multiply(0, 0)
         gather_scales(1, turns, "w_raw_0_0")
@@ -225,8 +227,7 @@ def tile_picked_merge_lin_bias_sub_e_kernel(tc, xT, w, b, offs, out):
         for m, name in ((1, "w_last"), (0, "w_raw_2_0")):
             last[m] = turns.tile([P, P, PACK], BF16, name=name, align_bytes=64)
         cast_on_scalar(last[1][:], w_raw[2, 1][:, :, P:])
-        cast_on_vector(last[0][:, :64, :], w_raw[2, 1][:, :, :64])
-        cast_on_scalar(last[0][:, 64:, :], w_raw[2, 1][:, :, 64:P])
+        cast_on_scalar(last[0][:], w_raw[2, 1][:, :, :P])
         for m in (1, 0):
             m_cols = slice(m * P, (m + 1) * P)
             quantize(w_codes[2, 1][:, m_cols], w_scales[2, 1][:, m_cols], last[m][:])

@@ -26,6 +26,7 @@ X_VECTOR = 544
 RUN = 2
 M_TILES = N // P
 PIECES = ((0, 256), (256, 384))
+ALIGN = 256
 
 
 def tile_picked_merge_lin_bias_sub_e_kernel(tc, xT, w, b, offs, out):
@@ -43,32 +44,32 @@ def tile_picked_merge_lin_bias_sub_e_kernel(tc, xT, w, b, offs, out):
         make_identity(nc, identity[:])
         bias_turned = psum.tile([P, P], F32, name="bias_turned")
         nc.tensor.transpose(bias_turned[:], bias_rows[:], identity[:])
-        x_scales = keep.tile([P, T], U8, name="x_scales", align_bytes=64)
+        x_scales = keep.tile([P, T], U8, name="x_scales", align_bytes=ALIGN)
         nc.gpsimd.memset(x_scales[:], 0)
 
         x_raw = {}
         w_raw = {}
 
         def load_x(c, t0, t1):
-            raw = turns.tile([P, PACK, t1 - t0], F32, name=f"x_raw_{c}_{t0}")
+            raw = turns.tile([P, PACK, t1 - t0], F32, name=f"x_raw_{c}_{t0}", align_bytes=ALIGN)
             rows = xT[c * K_PASS : (c + 1) * K_PASS, t0:t1]
             nc.sync.dma_start(out=raw[:], in_=rows.rearrange("(p j) w -> p j w", j=PACK))
             x_raw[c, t0] = raw
 
         def load_w(c, d):
-            w_raw[c, d] = turns.tile([P, PACK, N], F32, name=f"w_raw_{c}_{d}", align_bytes=64)
+            w_raw[c, d] = turns.tile([P, PACK, N], F32, name=f"w_raw_{c}_{d}", align_bytes=ALIGN)
             rows = w[d, c * K_PASS : (c + 1) * K_PASS, :]
             nc.sync.dma_start(out=w_raw[c, d][:], in_=rows.rearrange("(p j) n -> p j n", j=PACK))
 
         load_x(0, 0, T)
         nc.sync.dma_start(offsets[:], offs)
-        raw = turns.tile([P, PACK * T], F32, name="x_raw_1_0")
+        raw = turns.tile([P, PACK * T], F32, name="x_raw_1_0", align_bytes=ALIGN)
         rows = xT[K_PASS : 2 * K_PASS, :].rearrange("(p j) w -> p (j w)", j=PACK)
         cut = (PACK - 1) * T + 256
         nc.sync.dma_start(out=raw[:, :cut], in_=rows[:, :cut])
         nc.sync.dma_start(out=raw[:, cut:], in_=rows[:, cut:])
         x_raw[1, 0] = raw[:].rearrange("p (j w) -> p j w", j=PACK)
-        split = keep.tile([P, 2, 2, 2 * T], F32, name="x_raw_2", align_bytes=64)
+        split = keep.tile([P, 2, 2, 2 * T], F32, name="x_raw_2", align_bytes=ALIGN)
         rows = xT[2 * K_PASS :, :].rearrange("(p u e) w -> p u (e w)", u=2, e=2)
         nc.sync.dma_start(out=split[:, 0, :, : T + EARLY], in_=rows[:, :, : T + EARLY])
         nc.sync.dma_start(out=split[:, 1, :, EARLY:T], in_=rows[:, :, T + EARLY :])
@@ -94,8 +95,8 @@ def tile_picked_merge_lin_bias_sub_e_kernel(tc, xT, w, b, offs, out):
         def quantize(codes, scales, grouped):
             nc.vector.quantize_mx(out=codes.bitcast(FP8X4), scales=scales, in_=grouped.rearrange("p w j -> p (w j)"))
 
-        x_bf = [keep.tile([P, T, PACK], BF16, name=f"x_bf_{c}", align_bytes=64) for c in range(PASSES)]
-        x_codes = [keep.tile([P, T], U32, name=f"x_codes_{c}", align_bytes=64) for c in range(PASSES)]
+        x_bf = [keep.tile([P, T, PACK], BF16, name=f"x_bf_{c}", align_bytes=ALIGN) for c in range(PASSES)]
+        x_codes = [keep.tile([P, T], U32, name=f"x_codes_{c}", align_bytes=ALIGN) for c in range(PASSES)]
         g_codes = {}
         g_scales = {}
 
@@ -107,13 +108,13 @@ def tile_picked_merge_lin_bias_sub_e_kernel(tc, xT, w, b, offs, out):
             quantize(x_codes[c][:, t0:t1], x_scales[4 * c : P, t0:t1], x_bf[c][:, t0:t1, :])
 
         def gather_pass(c):
-            picked = keep.tile([P, S], U32, name=f"g_codes_{c}", align_bytes=64)
+            picked = keep.tile([P, S], U32, name=f"g_codes_{c}", align_bytes=ALIGN)
             nc.vector.tensor_copy(out=picked[:], in_=x_codes[c][:].indirect(offsets[:]))
             for d in range(D):
                 g_codes[c, d] = picked[:, d * V : (d + 1) * V]
 
         def gather_piece(c, d, name):
-            picked = turns.tile([P, V], U32, name=name, align_bytes=64)
+            picked = turns.tile([P, V], U32, name=name, align_bytes=ALIGN)
             piece = offsets[:, d * V // 16 : (d + 1) * V // 16]
             nc.vector.tensor_copy(out=picked[:], in_=x_codes[c][:].indirect(piece))
             g_codes[c, d] = picked[:]
@@ -123,14 +124,14 @@ def tile_picked_merge_lin_bias_sub_e_kernel(tc, xT, w, b, offs, out):
         w_scales = {}
 
         def cast_w(c, d, cut=N):
-            w_bf[c, d] = keep.tile([P, N, PACK], BF16, name=f"w_bf_{c}_{d}", align_bytes=64)
+            w_bf[c, d] = keep.tile([P, N, PACK], BF16, name=f"w_bf_{c}_{d}", align_bytes=ALIGN)
             cast_on_scalar(w_bf[c, d][:, :cut, :], w_raw[c, d][:, :, :cut])
             if cut < N:
                 cast_on_vector(w_bf[c, d][:, cut:, :], w_raw[c, d][:, :, cut:])
 
         def w_tiles(c, d):
-            w_codes[c, d] = keep.tile([P, N], U32, name=f"w_codes_{c}_{d}", align_bytes=64)
-            w_scales[c, d] = keep.tile([P, N], U8, name=f"w_scales_{c}_{d}", align_bytes=64)
+            w_codes[c, d] = keep.tile([P, N], U32, name=f"w_codes_{c}_{d}", align_bytes=ALIGN)
+            w_scales[c, d] = keep.tile([P, N], U8, name=f"w_scales_{c}_{d}", align_bytes=ALIGN)
 
         def quantize_w(c, d):
             w_tiles(c, d)
@@ -170,7 +171,7 @@ def tile_picked_merge_lin_bias_sub_e_kernel(tc, xT, w, b, offs, out):
         for t0 in (0, 256, 768, 512):
             quantize_x(1, t0, t0 + 256)
         gather_pass(1)
-        bias = turns.tile([P, M_TILES], F32, name="x_raw_1_0")
+        bias = turns.tile([P, M_TILES], F32, name="x_raw_1_0", align_bytes=ALIGN)
         nc.scalar.copy(out=bias[:], in_=bias_turned[:, :M_TILES])
         cast_x(2, 0, 256, cast_on_scalar)
         cast_x(2, 256, EARLY, cast_on_scalar)
@@ -192,11 +193,11 @@ def tile_picked_merge_lin_bias_sub_e_kernel(tc, xT, w, b, offs, out):
         quantize_x(2, 768, T)
 
         def gather_scales(d, pool, name):
-            g_scales[d] = pool.tile([P, V], U8, name=name, align_bytes=64)
+            g_scales[d] = pool.tile([P, V], U8, name=name, align_bytes=ALIGN)
             piece = offsets[:, d * V // 16 : (d + 1) * V // 16]
             nc.vector.tensor_copy(out=g_scales[d][:], in_=x_scales[:].indirect(piece))
 
-        w_bf[0, 0] = keep.tile([P, N, PACK], BF16, name="x_raw_2", align_bytes=64)
+        w_bf[0, 0] = keep.tile([P, N, PACK], BF16, name="x_raw_2", align_bytes=ALIGN)
         cast_on_vector(w_bf[0, 0][:, :96, :], w_raw[0, 0][:, :, :96])
         cast_on_scalar(w_bf[0, 0][:, 96:, :], w_raw[0, 0][:, :, 96:])
         gather_scales(0, keep, "g_scales_0")
@@ -217,7 +218,7 @@ def tile_picked_merge_lin_bias_sub_e_kernel(tc, xT, w, b, offs, out):
         w_tiles(2, 0)
         for m in (1, 0):
             m_cols = slice(m * P, (m + 1) * P)
-            half = keep.tile([P, P, PACK], BF16, name=f"w_half_{m}", align_bytes=64)
+            half = keep.tile([P, P, PACK], BF16, name=f"w_half_{m}", align_bytes=ALIGN)
             cast_on_scalar(half[:], w_raw[2, 0][:, :, m_cols])
             quantize(w_codes[2, 0][:, m_cols], w_scales[2, 0][:, m_cols], half[:])
         multiply(2, 0)
@@ -225,7 +226,7 @@ def tile_picked_merge_lin_bias_sub_e_kernel(tc, xT, w, b, offs, out):
         w_tiles(2, 1)
         last = {}
         for m, name in ((1, "w_last"), (0, "w_raw_2_0")):
-            last[m] = turns.tile([P, P, PACK], BF16, name=name, align_bytes=64)
+            last[m] = turns.tile([P, P, PACK], BF16, name=name, align_bytes=ALIGN)
         cast_on_scalar(last[1][:], w_raw[2, 1][:, :, P:])
         cast_on_scalar(last[0][:], w_raw[2, 1][:, :, :P])
         for m in (1, 0):
@@ -235,7 +236,7 @@ def tile_picked_merge_lin_bias_sub_e_kernel(tc, xT, w, b, offs, out):
 
         for m in (1, 0):
             for i, (v0, v1) in enumerate(PIECES):
-                result = keep.tile([P, v1 - v0], F32, name=f"result_{m}_{i}")
+                result = keep.tile([P, v1 - v0], F32, name=f"result_{m}_{i}", align_bytes=ALIGN)
                 if m != i:
                     nc.scalar.activation(out=result[:], in_=acc[m, i][:], func=IDENTITY, bias=bias[:, m : m + 1])
                     queue = nc.scalar

@@ -20,13 +20,12 @@ P = 128
 PACK = 4
 K_PASS = P * PACK
 PASSES = K // K_PASS
-HALF = T // 2
-EARLY = 384
-X_VECTOR = 544
+X_LOADS = (((0, 512), (512, T)), ((0, 512), (512, T)), ((0, 512), (512, 768), (768, T)))
 RUN = 2
 M_TILES = N // P
 PIECES = ((0, 256), (256, 384))
 ALIGN = 256
+LAST_SCALAR = 96
 
 
 def tile_picked_merge_lin_bias_sub_e_kernel(tc, xT, w, b, offs, out):
@@ -61,19 +60,11 @@ def tile_picked_merge_lin_bias_sub_e_kernel(tc, xT, w, b, offs, out):
             rows = w[d, c * K_PASS : (c + 1) * K_PASS, :]
             nc.sync.dma_start(out=w_raw[c, d][:], in_=rows.rearrange("(p j) n -> p j n", j=PACK))
 
-        load_x(0, 0, T)
-        nc.sync.dma_start(offsets[:], offs)
-        raw = turns.tile([P, PACK * T], F32, name="x_raw_1_0", align_bytes=ALIGN)
-        rows = xT[K_PASS : 2 * K_PASS, :].rearrange("(p j) w -> p (j w)", j=PACK)
-        cut = (PACK - 1) * T + 256
-        nc.sync.dma_start(out=raw[:, :cut], in_=rows[:, :cut])
-        nc.sync.dma_start(out=raw[:, cut:], in_=rows[:, cut:])
-        x_raw[1, 0] = raw[:].rearrange("p (j w) -> p j w", j=PACK)
-        split = keep.tile([P, 2, 2, 2 * T], F32, name="x_raw_2", align_bytes=ALIGN)
-        rows = xT[2 * K_PASS :, :].rearrange("(p u e) w -> p u (e w)", u=2, e=2)
-        nc.sync.dma_start(out=split[:, 0, :, : T + EARLY], in_=rows[:, :, : T + EARLY])
-        nc.sync.dma_start(out=split[:, 1, :, EARLY:T], in_=rows[:, :, T + EARLY :])
-        x_raw[2, 0] = split[:, 0, :, :].rearrange("p u (e w) -> p (u e) w", e=2)
+        for c in range(PASSES):
+            for t0, t1 in X_LOADS[c]:
+                load_x(c, t0, t1)
+                if (c, t0) == (0, 0):
+                    nc.sync.dma_start(offsets[:], offs)
         for c in range(PASSES):
             for d in range(D):
                 load_w(c, d)
@@ -101,7 +92,7 @@ def tile_picked_merge_lin_bias_sub_e_kernel(tc, xT, w, b, offs, out):
         g_scales = {}
 
         def cast_x(c, t0, t1, cast):
-            first = HALF if (c, HALF) in x_raw and t0 >= HALF else 0
+            first = max(a for a, z in X_LOADS[c] if a <= t0)
             cast(x_bf[c][:, t0:t1, :], x_raw[c, first][:, :, t0 - first : t1 - first])
 
         def quantize_x(c, t0, t1):
@@ -156,40 +147,33 @@ def tile_picked_merge_lin_bias_sub_e_kernel(tc, xT, w, b, offs, out):
                         stop=(c == PASSES - 1 and d == D - 1),
                     )
 
-        for c in range(1):
-            cast_x(c, 0, X_VECTOR, cast_on_vector)
-            cast_x(c, 768, T, cast_on_scalar)
-            cast_x(c, X_VECTOR, 768, cast_on_scalar)
-            quantize_x(c, 768, T)
-            quantize_x(c, 0, 512)
-            quantize_x(c, 512, 768)
-            gather_pass(c)
+        for t0 in (0, 512):
+            cast_x(0, t0, t0 + 320, cast_on_vector)
+            cast_x(0, t0 + 320, t0 + 512, cast_on_scalar)
+            quantize_x(0, t0, t0 + 256)
+            quantize_x(0, t0 + 256, t0 + 512)
+        gather_pass(0)
+        bias = turns.tile([P, M_TILES], F32, name="x_raw_0_512", align_bytes=ALIGN)
+        nc.scalar.copy(out=bias[:], in_=bias_turned[:, :M_TILES])
+
         cast_x(1, 0, 256, cast_on_scalar)
-        cast_x(1, 256, 640, cast_on_vector)
-        cast_x(1, 768, T, cast_on_scalar)
-        cast_x(1, 640, 768, cast_on_scalar)
-        for t0 in (0, 256, 768, 512):
+        cast_x(1, 256, 384, cast_on_scalar)
+        cast_x(1, 384, 512, cast_on_vector)
+        quantize_x(1, 0, 256)
+        cast_x(1, 512, 832, cast_on_vector)
+        cast_x(1, 832, T, cast_on_scalar)
+        for t0 in (256, 512, 768):
             quantize_x(1, t0, t0 + 256)
         gather_pass(1)
-        bias = turns.tile([P, M_TILES], F32, name="x_raw_1_0", align_bytes=ALIGN)
-        nc.scalar.copy(out=bias[:], in_=bias_turned[:, :M_TILES])
+
         cast_x(2, 0, 256, cast_on_scalar)
-        cast_x(2, 256, EARLY, cast_on_scalar)
+        cast_x(2, 256, 512, cast_on_scalar)
+        cast_x(2, 512, 768, cast_on_vector)
         quantize_x(2, 0, 256)
-
-        def late_views(t0, t1):
-            return (
-                x_bf[2][:, t0:t1, :].rearrange("p (c i) (u e) -> p c u e i", i=RUN, e=2),
-                split[:, :, :, t0:t1].rearrange("p e u (c i) -> p c u e i", i=RUN),
-            )
-
-        out_view, in_view = late_views(EARLY, 768)
-        nc.vector.tensor_copy(out=out_view, in_=in_view)
-        out_view, in_view = late_views(768, T)
-        nc.scalar.copy(out=out_view, in_=in_view)
-        quantize_x(2, 256, EARLY)
-        quantize_x(2, EARLY, 640)
-        quantize_x(2, 640, 768)
+        quantize_x(2, 512, 768)
+        cast_x(2, 768, 896, cast_on_vector)
+        cast_x(2, 896, T, cast_on_scalar)
+        quantize_x(2, 256, 512)
         quantize_x(2, 768, T)
 
         def gather_scales(d, pool, name):
@@ -197,9 +181,7 @@ def tile_picked_merge_lin_bias_sub_e_kernel(tc, xT, w, b, offs, out):
             piece = offsets[:, d * V // 16 : (d + 1) * V // 16]
             nc.vector.tensor_copy(out=g_scales[d][:], in_=x_scales[:].indirect(piece))
 
-        w_bf[0, 0] = keep.tile([P, N, PACK], BF16, name="x_raw_2", align_bytes=ALIGN)
-        cast_on_vector(w_bf[0, 0][:, :96, :], w_raw[0, 0][:, :, :96])
-        cast_on_scalar(w_bf[0, 0][:, 96:, :], w_raw[0, 0][:, :, 96:])
+        cast_w(0, 0)
         gather_scales(0, keep, "g_scales_0")
         quantize_w(0, 0)
         multiply(0, 0)
@@ -211,24 +193,19 @@ def tile_picked_merge_lin_bias_sub_e_kernel(tc, xT, w, b, offs, out):
         cast_w(1, 0)
         quantize_w(1, 0)
         multiply(1, 0)
+        gather_piece(2, 1, "w_raw_1_0")
         cast_w(1, 1)
         quantize_w(1, 1)
         multiply(1, 1)
-        gather_piece(2, 1, "w_raw_1_1")
-        w_tiles(2, 0)
-        for m in (1, 0):
-            m_cols = slice(m * P, (m + 1) * P)
-            half = keep.tile([P, P, PACK], BF16, name=f"w_half_{m}", align_bytes=ALIGN)
-            cast_on_scalar(half[:], w_raw[2, 0][:, :, m_cols])
-            quantize(w_codes[2, 0][:, m_cols], w_scales[2, 0][:, m_cols], half[:])
+        cast_w(2, 0)
+        quantize_w(2, 0)
         multiply(2, 0)
 
         w_tiles(2, 1)
-        last = {}
-        for m, name in ((1, "w_last"), (0, "w_raw_2_0")):
-            last[m] = turns.tile([P, P, PACK], BF16, name=name, align_bytes=ALIGN)
-        cast_on_scalar(last[1][:], w_raw[2, 1][:, :, P:])
-        cast_on_scalar(last[0][:], w_raw[2, 1][:, :, :P])
+        last = {m: keep.tile([P, P, PACK], BF16, name=f"w_last_{m}", align_bytes=ALIGN) for m in (1, 0)}
+        cast_on_vector(last[1][:], w_raw[2, 1][:, :, P:])
+        cast_on_vector(last[0][:, LAST_SCALAR:, :], w_raw[2, 1][:, :, LAST_SCALAR:P])
+        cast_on_scalar(last[0][:, :LAST_SCALAR, :], w_raw[2, 1][:, :, :LAST_SCALAR])
         for m in (1, 0):
             m_cols = slice(m * P, (m + 1) * P)
             quantize(w_codes[2, 1][:, m_cols], w_scales[2, 1][:, m_cols], last[m][:])

@@ -20,12 +20,13 @@ P = 128
 PACK = 4
 K_PASS = P * PACK
 PASSES = K // K_PASS
-X_LOADS = (((0, 512), (512, T)), ((0, 512), (512, T)), ((0, 512), (512, 768), (768, T)))
+HALF = T // 2
+LAST_SCALAR = 64
+X_VECTOR = 544
 RUN = 2
 M_TILES = N // P
 PIECES = ((0, 256), (256, 384))
 ALIGN = 256
-LAST_SCALAR = 96
 
 
 def tile_picked_merge_lin_bias_sub_e_kernel(tc, xT, w, b, offs, out):
@@ -60,11 +61,11 @@ def tile_picked_merge_lin_bias_sub_e_kernel(tc, xT, w, b, offs, out):
             rows = w[d, c * K_PASS : (c + 1) * K_PASS, :]
             nc.sync.dma_start(out=w_raw[c, d][:], in_=rows.rearrange("(p j) n -> p j n", j=PACK))
 
-        for c in range(PASSES):
-            for t0, t1 in X_LOADS[c]:
-                load_x(c, t0, t1)
-                if (c, t0) == (0, 0):
-                    nc.sync.dma_start(offsets[:], offs)
+        load_x(0, 0, T)
+        nc.sync.dma_start(offsets[:], offs)
+        for c in range(1, PASSES):
+            load_x(c, 0, HALF)
+            load_x(c, HALF, T)
         for c in range(PASSES):
             for d in range(D):
                 load_w(c, d)
@@ -92,7 +93,7 @@ def tile_picked_merge_lin_bias_sub_e_kernel(tc, xT, w, b, offs, out):
         g_scales = {}
 
         def cast_x(c, t0, t1, cast):
-            first = max(a for a, z in X_LOADS[c] if a <= t0)
+            first = HALF if (c, HALF) in x_raw and t0 >= HALF else 0
             cast(x_bf[c][:, t0:t1, :], x_raw[c, first][:, :, t0 - first : t1 - first])
 
         def quantize_x(c, t0, t1):
@@ -147,34 +148,33 @@ def tile_picked_merge_lin_bias_sub_e_kernel(tc, xT, w, b, offs, out):
                         stop=(c == PASSES - 1 and d == D - 1),
                     )
 
-        for t0 in (0, 512):
-            cast_x(0, t0, t0 + 320, cast_on_vector)
-            cast_x(0, t0 + 320, t0 + 512, cast_on_scalar)
-            quantize_x(0, t0, t0 + 256)
-            quantize_x(0, t0 + 256, t0 + 512)
-        gather_pass(0)
-        bias = turns.tile([P, M_TILES], F32, name="x_raw_0_512", align_bytes=ALIGN)
+        for c in range(1):
+            cast_x(c, 0, X_VECTOR, cast_on_vector)
+            cast_x(c, 768, T, cast_on_scalar)
+            cast_x(c, X_VECTOR, 768, cast_on_scalar)
+            quantize_x(c, 768, T)
+            quantize_x(c, 0, 512)
+            quantize_x(c, 512, 768)
+            gather_pass(c)
+        bias = turns.tile([P, M_TILES], F32, name="x_raw_0_0", align_bytes=ALIGN)
         nc.scalar.copy(out=bias[:], in_=bias_turned[:, :M_TILES])
 
         cast_x(1, 0, 256, cast_on_scalar)
-        cast_x(1, 256, 384, cast_on_scalar)
-        cast_x(1, 384, 512, cast_on_vector)
-        quantize_x(1, 0, 256)
-        cast_x(1, 512, 832, cast_on_vector)
-        cast_x(1, 832, T, cast_on_scalar)
-        for t0 in (256, 512, 768):
+        cast_x(1, 256, HALF, cast_on_scalar)
+        cast_x(1, HALF, 704, cast_on_vector)
+        cast_x(1, 768, T, cast_on_scalar)
+        cast_x(1, 704, 768, cast_on_scalar)
+        for t0 in (0, 256, 768, 512):
             quantize_x(1, t0, t0 + 256)
         gather_pass(1)
 
         cast_x(2, 0, 256, cast_on_scalar)
-        cast_x(2, 256, 512, cast_on_scalar)
-        cast_x(2, 512, 768, cast_on_vector)
+        cast_x(2, 256, HALF, cast_on_scalar)
         quantize_x(2, 0, 256)
-        quantize_x(2, 512, 768)
-        cast_x(2, 768, 896, cast_on_vector)
-        cast_x(2, 896, T, cast_on_scalar)
-        quantize_x(2, 256, 512)
-        quantize_x(2, 768, T)
+        cast_x(2, HALF, 768, cast_on_vector)
+        cast_x(2, 768, T, cast_on_scalar)
+        for t0 in (256, 512, 768):
+            quantize_x(2, t0, t0 + 256)
 
         def gather_scales(d, pool, name):
             g_scales[d] = pool.tile([P, V], U8, name=name, align_bytes=ALIGN)
@@ -193,17 +193,23 @@ def tile_picked_merge_lin_bias_sub_e_kernel(tc, xT, w, b, offs, out):
         cast_w(1, 0)
         quantize_w(1, 0)
         multiply(1, 0)
-        gather_piece(2, 1, "w_raw_1_0")
         cast_w(1, 1)
         quantize_w(1, 1)
         multiply(1, 1)
-        cast_w(2, 0)
-        quantize_w(2, 0)
+        gather_piece(2, 1, "w_raw_1_1")
+        w_tiles(2, 0)
+        for m in (1, 0):
+            m_cols = slice(m * P, (m + 1) * P)
+            half = keep.tile([P, P, PACK], BF16, name=f"w_half_{m}", align_bytes=ALIGN)
+            cast_on_scalar(half[:], w_raw[2, 0][:, :, m_cols])
+            quantize(w_codes[2, 0][:, m_cols], w_scales[2, 0][:, m_cols], half[:])
         multiply(2, 0)
 
         w_tiles(2, 1)
-        last = {m: keep.tile([P, P, PACK], BF16, name=f"w_last_{m}", align_bytes=ALIGN) for m in (1, 0)}
-        cast_on_vector(last[1][:], w_raw[2, 1][:, :, P:])
+        last = {}
+        for m, name in ((1, "w_last"), (0, "w_raw_2_0")):
+            last[m] = turns.tile([P, P, PACK], BF16, name=name, align_bytes=ALIGN)
+        cast_on_scalar(last[1][:], w_raw[2, 1][:, :, P:])
         cast_on_vector(last[0][:, LAST_SCALAR:, :], w_raw[2, 1][:, :, LAST_SCALAR:P])
         cast_on_scalar(last[0][:, :LAST_SCALAR, :], w_raw[2, 1][:, :, :LAST_SCALAR])
         for m in (1, 0):

@@ -27,6 +27,7 @@ RUN = 2
 M_TILES = N // P
 PIECES = ((0, 256), (256, 384))
 ALIGN = 256
+LATE = 128
 
 
 def tile_picked_merge_lin_bias_sub_e_kernel(tc, xT, w, b, offs, out):
@@ -63,9 +64,14 @@ def tile_picked_merge_lin_bias_sub_e_kernel(tc, xT, w, b, offs, out):
 
         load_x(0, 0, T)
         nc.sync.dma_start(offsets[:], offs)
-        for c in range(1, PASSES):
-            load_x(c, 0, HALF)
-            load_x(c, HALF, T)
+        raw = turns.tile([P, PACK * T], F32, name="x_raw_1_0", align_bytes=ALIGN)
+        rows = xT[K_PASS : 2 * K_PASS, :].rearrange("(p j) w -> p (j w)", j=PACK)
+        cut = (PACK - 1) * T + 256
+        nc.sync.dma_start(out=raw[:, :cut], in_=rows[:, :cut])
+        nc.sync.dma_start(out=raw[:, cut:], in_=rows[:, cut:])
+        x_raw[1, 0] = raw[:].rearrange("p (j w) -> p j w", j=PACK)
+        load_x(2, 0, HALF)
+        load_x(2, HALF, T)
         for c in range(PASSES):
             for d in range(D):
                 load_w(c, d)
@@ -134,6 +140,11 @@ def tile_picked_merge_lin_bias_sub_e_kernel(tc, xT, w, b, offs, out):
             for i, (v0, v1) in enumerate(PIECES):
                 acc[m, i] = psum.tile([P, v1 - v0], F32, name=f"acc_{m}_{i}")
 
+        def moving(c, d, v0, v1):
+            if (c, d) == (1, 1):
+                return g_late[:] if v0 else g_wide
+            return g_codes[c, d][:, v0:v1]
+
         def multiply(c, d):
             for m in (1, 0):
                 m_cols = slice(m * P, (m + 1) * P)
@@ -142,7 +153,7 @@ def tile_picked_merge_lin_bias_sub_e_kernel(tc, xT, w, b, offs, out):
                         out=acc[m, i][:],
                         lhsT=w_codes[c, d][:, m_cols].bitcast(FP8X4),
                         lhsT_scale=w_scales[c, d][:, m_cols],
-                        rhs=g_codes[c, d][:, v0:v1].bitcast(FP8X4),
+                        rhs=moving(c, d, v0, v1).bitcast(FP8X4),
                         rhs_scale=g_scales[d][4 * c : P, v0:v1],
                         start=(c == 0 and d == 0),
                         stop=(c == PASSES - 1 and d == D - 1),
@@ -156,17 +167,18 @@ def tile_picked_merge_lin_bias_sub_e_kernel(tc, xT, w, b, offs, out):
             quantize_x(c, 0, 512)
             quantize_x(c, 512, 768)
             gather_pass(c)
-        bias = turns.tile([P, M_TILES], F32, name="x_raw_0_0", align_bytes=ALIGN)
-        nc.scalar.copy(out=bias[:], in_=bias_turned[:, :M_TILES])
-
         cast_x(1, 0, 256, cast_on_scalar)
-        cast_x(1, 256, HALF, cast_on_scalar)
-        cast_x(1, HALF, 704, cast_on_vector)
+        cast_x(1, 256, 640, cast_on_vector)
         cast_x(1, 768, T, cast_on_scalar)
-        cast_x(1, 704, 768, cast_on_scalar)
+        cast_x(1, 640, 768, cast_on_scalar)
         for t0 in (0, 256, 768, 512):
             quantize_x(1, t0, t0 + 256)
-        gather_pass(1)
+        picked = keep.tile([P, S - LATE], U32, name="g_codes_1", align_bytes=ALIGN)
+        nc.vector.tensor_copy(out=picked[:], in_=x_codes[1][:].indirect(offsets[:, : (S - LATE) // 16]))
+        g_codes[1, 0] = picked[:, :V]
+        g_wide = picked[:, V:]
+        bias = turns.tile([P, M_TILES], F32, name="x_raw_1_0", align_bytes=ALIGN)
+        nc.scalar.copy(out=bias[:], in_=bias_turned[:, :M_TILES])
 
         cast_x(2, 0, 256, cast_on_scalar)
         cast_x(2, 256, HALF, cast_on_scalar)
@@ -181,6 +193,8 @@ def tile_picked_merge_lin_bias_sub_e_kernel(tc, xT, w, b, offs, out):
             piece = offsets[:, d * V // 16 : (d + 1) * V // 16]
             nc.vector.tensor_copy(out=g_scales[d][:], in_=x_scales[:].indirect(piece))
 
+        g_late = turns.tile([P, LATE], U32, name="x_raw_2_512", align_bytes=ALIGN)
+        nc.vector.tensor_copy(out=g_late[:], in_=x_codes[1][:].indirect(offsets[:, (S - LATE) // 16 :]))
         cast_w(0, 0)
         gather_scales(0, keep, "g_scales_0")
         quantize_w(0, 0)

@@ -1,7 +1,6 @@
 from contextlib import ExitStack
 
 import concourse.mybir as mybir
-from concourse.masks import make_identity
 
 K, T, D, S, V, N = 1536, 1024, 2, 768, 384, 256
 FLOPS = 2 * N * V * D * K
@@ -38,15 +37,8 @@ def tile_picked_merge_lin_bias_sub_e_kernel(tc, xT, w, b, offs, out):
         psum = ctx.enter_context(tc.psum_pool(name="psum", bufs=1))
 
         offsets = keep.tile([P, S // 16], U16, name="offsets")
-        bias_rows = keep.tile([P, P], F32, name="bias_rows")
-        nc.gpsimd.memset(bias_rows[:], 0.0)
-        nc.scalar.dma_start(out=bias_rows[:M_TILES, :], in_=b.rearrange("(c p) o -> c (p o)", p=P))
-        identity = keep.tile([P, P], F32, name="identity")
-        make_identity(nc, identity[:])
-        bias_turned = psum.tile([P, P], F32, name="bias_turned")
-        nc.tensor.transpose(bias_turned[:], bias_rows[:], identity[:])
         x_scales = keep.tile([P, T], U8, name="x_scales", align_bytes=ALIGN)
-        nc.gpsimd.memset(x_scales[:], 0)
+        nc.vector.memset(x_scales[:].bitcast(U32), 0)
 
         x_raw = {}
         w_raw = {}
@@ -75,6 +67,9 @@ def tile_picked_merge_lin_bias_sub_e_kernel(tc, xT, w, b, offs, out):
         for c in range(PASSES):
             for d in range(D):
                 load_w(c, d)
+        bias = keep.tile([P, M_TILES], F32, name="bias", align_bytes=ALIGN)
+        with nc.allow_non_contiguous_dma(reason="one bias value for each partition and output tile"):
+            nc.sync.dma_start(out=bias[:], in_=b.rearrange("(m p) o -> p (m o)", p=P))
 
         def views(dst, raw):
             return (
@@ -177,8 +172,6 @@ def tile_picked_merge_lin_bias_sub_e_kernel(tc, xT, w, b, offs, out):
         nc.vector.tensor_copy(out=picked[:], in_=x_codes[1][:].indirect(offsets[:, : (S - LATE) // 16]))
         g_codes[1, 0] = picked[:, :V]
         g_wide = picked[:, V:]
-        bias = turns.tile([P, M_TILES], F32, name="x_raw_1_0", align_bytes=ALIGN)
-        nc.scalar.copy(out=bias[:], in_=bias_turned[:, :M_TILES])
 
         cast_x(2, 0, 256, cast_on_scalar)
         cast_x(2, 256, HALF, cast_on_scalar)

@@ -181,18 +181,15 @@ def tile_picked_merge_lin_bias_sub_e_kernel(tc, xT, w, b, offs, out):
         for t0 in (256, 512, 768):
             quantize_x(2, t0, t0 + 256)
 
-        def gather_scales(d, pool, name):
-            g_scales[d] = pool.tile([P, V], U8, name=name, align_bytes=ALIGN)
-            piece = offsets[:, d * V // 16 : (d + 1) * V // 16]
-            nc.vector.tensor_copy(out=g_scales[d][:], in_=x_scales[:].indirect(piece))
-
         g_late = turns.tile([P, LATE], U32, name="x_raw_2_512", align_bytes=ALIGN)
         nc.vector.tensor_copy(out=g_late[:], in_=x_codes[1][:].indirect(offsets[:, (S - LATE) // 16 :]))
         cast_w(0, 0)
-        gather_scales(0, keep, "g_scales_0")
+        picked_scales = keep.tile([P, S], U8, name="g_scales", align_bytes=ALIGN)
+        nc.vector.tensor_copy(out=picked_scales[:], in_=x_scales[:].indirect(offsets[:]))
+        for d in range(D):
+            g_scales[d] = picked_scales[:, d * V : (d + 1) * V]
         quantize_w(0, 0)
         multiply(0, 0)
-        gather_scales(1, turns, "w_raw_0_0")
         cast_w(0, 1)
         quantize_w(0, 1)
         multiply(0, 1)

from contextlib import ExitStack

import concourse.mybir as mybir

K, T, D, S, V, N = 1536, 1024, 2, 768, 384, 256
FLOPS = 2 * N * V * D * K

F32 = mybir.dt.float32
BF16 = mybir.dt.bfloat16
U32 = mybir.dt.uint32
U16 = mybir.dt.uint16
U8 = mybir.dt.uint8
FP8X4 = mybir.dt.float8_e4m3fn_x4
COPY = mybir.ActivationFunctionType.Copy
IDENTITY = mybir.ActivationFunctionType.Identity
ADD = mybir.AluOpType.add

P = 128
PACK = 4
K_PASS = P * PACK
PASSES = K // K_PASS
HALF = T // 2
LAST_SCALAR = 64
X_VECTOR = 544
RUN = 2
M_TILES = N // P
PIECES = ((0, 256), (256, 384))
ALIGN = 256
LATE = 128


def tile_picked_merge_lin_bias_sub_e_kernel(tc, xT, w, b, offs, out):
    nc = tc.nc
    with ExitStack() as ctx:
        keep = ctx.enter_context(tc.tile_pool(name="keep", bufs=1))
        turns = ctx.enter_context(tc.tile_pool(name="turns", bufs=1))
        psum = ctx.enter_context(tc.psum_pool(name="psum", bufs=1))

        offsets = keep.tile([P, S // 16], U16, name="offsets")
        x_scales = keep.tile([P, T], U8, name="x_scales", align_bytes=ALIGN)
        nc.vector.memset(x_scales[:].bitcast(U32), 0)

        x_raw = {}
        w_raw = {}

        def load_x(c, t0, t1):
            raw = turns.tile([P, PACK, t1 - t0], F32, name=f"x_raw_{c}_{t0}", align_bytes=ALIGN)
            rows = xT[c * K_PASS : (c + 1) * K_PASS, t0:t1]
            nc.sync.dma_start(out=raw[:], in_=rows.rearrange("(p j) w -> p j w", j=PACK))
            x_raw[c, t0] = raw

        def load_w(c, d):
            w_raw[c, d] = turns.tile([P, PACK, N], F32, name=f"w_raw_{c}_{d}", align_bytes=ALIGN)
            rows = w[d, c * K_PASS : (c + 1) * K_PASS, :]
            nc.sync.dma_start(out=w_raw[c, d][:], in_=rows.rearrange("(p j) n -> p j n", j=PACK))

        load_x(0, 0, T)
        nc.sync.dma_start(offsets[:], offs)
        raw = turns.tile([P, PACK * T], F32, name="x_raw_1_0", align_bytes=ALIGN)
        rows = xT[K_PASS : 2 * K_PASS, :].rearrange("(p j) w -> p (j w)", j=PACK)
        cut = (PACK - 1) * T + 256
        nc.sync.dma_start(out=raw[:, :cut], in_=rows[:, :cut])
        nc.sync.dma_start(out=raw[:, cut:], in_=rows[:, cut:])
        x_raw[1, 0] = raw[:].rearrange("p (j w) -> p j w", j=PACK)
        load_x(2, 0, HALF)
        load_x(2, HALF, T)
        for c in range(PASSES):
            for d in range(D):
                load_w(c, d)
        bias = keep.tile([P, M_TILES], F32, name="bias", align_bytes=ALIGN)
        with nc.allow_non_contiguous_dma(reason="one bias value for each partition and output tile"):
            nc.sync.dma_start(out=bias[:], in_=b.rearrange("(m p) o -> p (m o)", p=P))

        def views(dst, raw):
            return (
                dst.rearrange("p (c i) t -> p c t i", i=RUN),
                raw.rearrange("p t (c i) -> p c t i", i=RUN),
            )

        def cast_on_scalar(dst, raw):
            out_view, in_view = views(dst, raw)
            nc.scalar.activation(out=out_view, in_=in_view, func=COPY)

        def cast_on_vector(dst, raw):
            out_view, in_view = views(dst, raw)
            nc.vector.tensor_copy(out=out_view, in_=in_view)

        def quantize(codes, scales, grouped):
            nc.vector.quantize_mx(out=codes.bitcast(FP8X4), scales=scales, in_=grouped.rearrange("p w j -> p (w j)"))

        x_bf = [keep.tile([P, T, PACK], BF16, name=f"x_bf_{c}", align_bytes=ALIGN) for c in range(PASSES)]
        x_codes = [keep.tile([P, T], U32, name=f"x_codes_{c}", align_bytes=ALIGN) for c in range(PASSES)]
        g_codes = {}
        g_scales = {}

        def cast_x(c, t0, t1, cast):
            first = HALF if (c, HALF) in x_raw and t0 >= HALF else 0
            cast(x_bf[c][:, t0:t1, :], x_raw[c, first][:, :, t0 - first : t1 - first])

        def quantize_x(c, t0, t1):
            quantize(x_codes[c][:, t0:t1], x_scales[4 * c : P, t0:t1], x_bf[c][:, t0:t1, :])

        def gather_pass(c):
            picked = keep.tile([P, S], U32, name=f"g_codes_{c}", align_bytes=ALIGN)
            nc.vector.tensor_copy(out=picked[:], in_=x_codes[c][:].indirect(offsets[:]))
            for d in range(D):
                g_codes[c, d] = picked[:, d * V : (d + 1) * V]

        def gather_piece(c, d, name):
            picked = turns.tile([P, V], U32, name=name, align_bytes=ALIGN)
            piece = offsets[:, d * V // 16 : (d + 1) * V // 16]
            nc.vector.tensor_copy(out=picked[:], in_=x_codes[c][:].indirect(piece))
            g_codes[c, d] = picked[:]

        w_bf = {}
        w_codes = {}
        w_scales = {}

        def cast_w(c, d, cut=N):
            w_bf[c, d] = keep.tile([P, N, PACK], BF16, name=f"w_bf_{c}_{d}", align_bytes=ALIGN)
            cast_on_scalar(w_bf[c, d][:, :cut, :], w_raw[c, d][:, :, :cut])
            if cut < N:
                cast_on_vector(w_bf[c, d][:, cut:, :], w_raw[c, d][:, :, cut:])

        def w_tiles(c, d):
            w_codes[c, d] = keep.tile([P, N], U32, name=f"w_codes_{c}_{d}", align_bytes=ALIGN)
            w_scales[c, d] = keep.tile([P, N], U8, name=f"w_scales_{c}_{d}", align_bytes=ALIGN)

        def quantize_w(c, d):
            w_tiles(c, d)
            quantize(w_codes[c, d][:], w_scales[c, d][:], w_bf[c, d][:])

        acc = {}
        for m in range(M_TILES):
            for i, (v0, v1) in enumerate(PIECES):
                acc[m, i] = psum.tile([P, v1 - v0], F32, name=f"acc_{m}_{i}")

        def moving(c, d, v0, v1):
            if (c, d) == (1, 1):
                return g_late[:] if v0 else g_wide
            return g_codes[c, d][:, v0:v1]

        def multiply(c, d):
            for m in (1, 0):
                m_cols = slice(m * P, (m + 1) * P)
                for i, (v0, v1) in enumerate(PIECES):
                    nc.tensor.matmul_mx(
                        out=acc[m, i][:],
                        lhsT=w_codes[c, d][:, m_cols].bitcast(FP8X4),
                        lhsT_scale=w_scales[c, d][:, m_cols],
                        rhs=moving(c, d, v0, v1).bitcast(FP8X4),
                        rhs_scale=g_scales[d][4 * c : P, v0:v1],
                        start=(c == 0 and d == 0),
                        stop=(c == PASSES - 1 and d == D - 1),
                    )

        for c in range(1):
            cast_x(c, 0, X_VECTOR, cast_on_vector)
            cast_x(c, 768, T, cast_on_scalar)
            cast_x(c, X_VECTOR, 768, cast_on_scalar)
            quantize_x(c, 768, T)
            quantize_x(c, 0, 512)
            quantize_x(c, 512, 768)
            gather_pass(c)
        cast_x(1, 0, 256, cast_on_scalar)
        cast_x(1, 256, 640, cast_on_vector)
        cast_x(1, 768, T, cast_on_scalar)
        cast_x(1, 640, 768, cast_on_scalar)
        for t0 in (0, 256, 768, 512):
            quantize_x(1, t0, t0 + 256)
        picked = keep.tile([P, S - LATE], U32, name="g_codes_1", align_bytes=ALIGN)
        nc.vector.tensor_copy(out=picked[:], in_=x_codes[1][:].indirect(offsets[:, : (S - LATE) // 16]))
        g_codes[1, 0] = picked[:, :V]
        g_wide = picked[:, V:]

        cast_x(2, 0, 256, cast_on_scalar)
        cast_x(2, 256, HALF, cast_on_scalar)
        quantize_x(2, 0, 256)
        cast_x(2, HALF, 768, cast_on_vector)
        cast_x(2, 768, T, cast_on_scalar)
        for t0 in (256, 512, 768):
            quantize_x(2, t0, t0 + 256)

        g_late = turns.tile([P, LATE], U32, name="x_raw_2_512", align_bytes=ALIGN)
        nc.vector.tensor_copy(out=g_late[:], in_=x_codes[1][:].indirect(offsets[:, (S - LATE) // 16 :]))
        cast_w(0, 0)
        picked_scales = keep.tile([P, S], U8, name="g_scales", align_bytes=ALIGN)
        nc.vector.tensor_copy(out=picked_scales[:], in_=x_scales[:].indirect(offsets[:]))
        for d in range(D):
            g_scales[d] = picked_scales[:, d * V : (d + 1) * V]
        quantize_w(0, 0)
        multiply(0, 0)
        cast_w(0, 1)
        quantize_w(0, 1)
        multiply(0, 1)
        gather_piece(2, 0, "w_raw_0_1")
        cast_w(1, 0)
        quantize_w(1, 0)
        multiply(1, 0)
        cast_w(1, 1)
        quantize_w(1, 1)
        multiply(1, 1)
        gather_piece(2, 1, "w_raw_1_1")
        w_tiles(2, 0)
        for m in (1, 0):
            m_cols = slice(m * P, (m + 1) * P)
            half = keep.tile([P, P, PACK], BF16, name=f"w_half_{m}", align_bytes=ALIGN)
            cast_on_scalar(half[:], w_raw[2, 0][:, :, m_cols])
            quantize(w_codes[2, 0][:, m_cols], w_scales[2, 0][:, m_cols], half[:])
        multiply(2, 0)

        w_tiles(2, 1)
        last = {}
        for m, name in ((1, "w_last"), (0, "w_raw_2_0")):
            last[m] = turns.tile([P, P, PACK], BF16, name=name, align_bytes=ALIGN)
        cast_on_scalar(last[1][:], w_raw[2, 1][:, :, P:])
        cast_on_vector(last[0][:, LAST_SCALAR:, :], w_raw[2, 1][:, :, LAST_SCALAR:P])
        cast_on_scalar(last[0][:, :LAST_SCALAR, :], w_raw[2, 1][:, :, :LAST_SCALAR])
        for m in (1, 0):
            m_cols = slice(m * P, (m + 1) * P)
            quantize(w_codes[2, 1][:, m_cols], w_scales[2, 1][:, m_cols], last[m][:])
        multiply(2, 1)

        for m in (1, 0):
            for i, (v0, v1) in enumerate(PIECES):
                result = keep.tile([P, v1 - v0], F32, name=f"result_{m}_{i}", align_bytes=ALIGN)
                if m != i:
                    nc.scalar.activation(out=result[:], in_=acc[m, i][:], func=IDENTITY, bias=bias[:, m : m + 1])
                    queue = nc.scalar
                else:
                    nc.vector.tensor_scalar(
                        out=result[:], in0=acc[m, i][:], scalar1=bias[:, m : m + 1], scalar2=None, op0=ADD
                    )
                    queue = nc.sync
                queue.dma_start(out=out[m * P : (m + 1) * P, v0:v1], in_=result[:])
